import numpy as np, ml_dtypes
CORES = [89,94,345,350]
N = 4
import mx_ref
NC, G = 128, 2
C = np.float32(0.031)
BF = ml_dtypes.bfloat16
def cut(t, i, w=512):
    return t[:, w * i:w * i + w]
def tile(rs):
    return np.stack(rs, axis=2).reshape(128, -1).astype(BF)
def layer(w, X):
    out = []
    for i in range(G):
        for t in range(len(X)):
            p = mx_ref.matmul(mx_ref.quantize(cut(w, len(X) * i + t)), X[t])
            z = p if t == 0 else z + p
        out.append(z)
    return out
def act(Z):
    return [np.maximum(s * z, 0) * C for z in Z for s in (1, -1)]
def setup_inputs(rng):
    def f(*shape):
        return mx_ref.flush((rng.standard_normal(shape, dtype=np.float32) * np.exp2(rng.integers(-2, 3, shape[:-1] + (1,)))).astype(BF))
    return {"xk": f(N, 128, 512), "xq": f(N, 128, 4 * NC), "wk": f(N, 128, G * 512), "wq": f(N, 128, G * 512)}
def setup_inputs_blocks(rng):
    d = setup_inputs(rng)
    for k in ("xk", "xq", "wk", "wq"): d[k] = mx_ref.spread(d[k], rng, 4)
    return d
def setup_inputs_wide(rng):
    d = setup_inputs(rng)
    for k in ("xk", "xq", "wk", "wq"): d[k] = mx_ref.flush((d[k].astype(np.float32) * np.exp2(rng.integers(-5, 6, (N, 1, 1))).astype(np.float32)).astype(BF))
    return d
def reference(xk, xq, wk, wq):
    K = [mx_ref.quantize(tile(act(layer(wk[j], [mx_ref.quantize(xk[j])])))) for j in range(N)]
    y = np.zeros((N, 128, N * NC), np.float32)
    for r in range(N):
        q = mx_ref.quantize(tile(act(layer(wq[r], [mx_ref.quantize(xq[r])]))))
        for j in range(N):
            y[r][:, NC * j:NC * j + NC] = mx_ref.matmul(K[j], q)
    return {"y": y}

@@ -1,0 +1,183 @@
+import numpy as np
+from concourse.bass import DstId, RemoteDMATransfer
+from concourse.mybir import dt, AluOpType, ActivationFunctionType
+
+NC = 128
+HOSTS = 4
+C = float(np.float32(0.031))
+
+PIECES = [(True, 0, NC, False), (False, 0, NC, True)]
+ENG_OFF = 8
+ENG_ON = 8
+
+SCRATCH = {
+    "xk_t": ("sbuf", [128, 512], "bfloat16"), "wk_t": ("sbuf", [128, 1024], "bfloat16"),
+    "xq_t": ("sbuf", [128, 512], "bfloat16"), "wq_t": ("sbuf", [128, 1024], "bfloat16"),
+    "xk_c": ("sbuf", [128, NC], "float8_e4m3fn_x4"), "xk_s": ("sbuf", [128, NC], "uint8"),
+    "xq_c": ("sbuf", [128, NC], "float8_e4m3fn_x4"), "xq_s": ("sbuf", [128, NC], "uint8"),
+    "wk_c": ("sbuf", [128, 2 * NC], "float8_e4m3fn_x4"), "wk_s": ("sbuf", [128, 2 * NC], "uint8"),
+    "wq_c": ("sbuf", [128, 2 * NC], "float8_e4m3fn_x4"), "wq_s": ("sbuf", [128, 2 * NC], "uint8"),
+    "k_t": ("sbuf", [128, 512], "bfloat16"), "q_t": ("sbuf", [128, 512], "bfloat16"),
+    "kc": ("sbuf", [128, 4 * NC], "float8_e4m3fn_x4"), "ks": ("sbuf", [128, 4 * NC], "uint8"),
+    "qc": ("sbuf", [128, NC], "float8_e4m3fn_x4"), "qs": ("sbuf", [128, NC], "uint8"),
+    "y_t": ("sbuf", [128, 4 * NC], "float32"),
+    "ps": ("psum", [128, 8 * 512], "float32"),
+}
+SEMAPHORES = ([s + n for n in "kq" for s in ("ld_x", "ld_w", "qx", "qw0", "qw1", "z0", "z1", "av", "as", "done")]
+              + [s + str(j) for s in ("arr", "y", "c", "st") for j in range(4)] + ["left"])
+
+
+def engines(mask, n, avoid=0):
+    free = [i for i in range(mask.bit_length()) if (mask >> i) & 1]
+    order = [i for i in free if not (avoid >> i) & 1] + [i for i in free if (avoid >> i) & 1]
+    m = 0
+    for i in order[:n]:
+        m |= 1 << i
+    return m
+
+
+def count(mask):
+    return bin(mask).count("1")
+
+
+def plan(cores, topo):
+    used = set(cores)
+    streams = []
+    for j, s in enumerate(cores):
+        far = [d for d in cores if d != s and not topo.may_write(s, d)]
+        if not far:
+            continue
+        for p, (_, _, _, own_rack) in enumerate(PIECES):
+            ok = [c for c in range(HOSTS * topo.CORES_PER_HOST)
+                  if c not in used and topo.chip(c) == topo.chip(s) and topo.die(c) == topo.die(s)
+                  and topo.may_write(s, c) and all(topo.may_write(c, d) for d in far)
+                  and (topo.same_plane(s, c) if own_rack else all(topo.same_plane(c, d) for d in far))]
+            used.add(ok[0])
+            streams.append((j, p, ok[0], far))
+    return streams
+
+
+def rank_program(g, core, T, topo):
+    cores = [int(c) for c in T.cores]
+    streams = plan(cores, topo)
+    S = T.sem
+    rank = T.rank_of(core)
+
+    def view(codes, j, lo, hi):
+        if codes:
+            return T.kc[:, NC * j + lo:NC * j + hi].bitcast(dt.uint8)
+        return T.ks[:, NC * j + lo:NC * j + hi]
+
+    def piece(p, j):
+        return view(PIECES[p][0], j, PIECES[p][1], PIECES[p][2])
+
+    def off_mask(src, dsts):
+        m = topo.mask(src, dsts[0])
+        for d in dsts[1:]:
+            m &= topo.mask(src, d)
+        return engines(m, ENG_OFF)
+
+    if rank is None:
+        for j, p, relay, far in streams:
+            if relay != core:
+                continue
+            m = off_mask(core, far)
+            ids = [DstId(rid=topo.addr(d, core)[0], pnc=topo.addr(d, core)[1]) for d in far]
+            g.wait_ge(S["arr%d" % j], count(off_mask(cores[j], [relay])))
+            g.remote_dma_fused([RemoteDMATransfer(dst_ids=ids, dma_engine_mask=m, remote_sem=S["arr%d" % j],
+                                                  srcs=[piece(p, j)], dsts=[piece(p, j) for _ in far])],
+                               local_sem=S.left)
+            g.wait_ge(S.left, count(m))
+        return
+
+    v, a, t, sy = g.vector, g.scalar, g.tensor, g.sync
+    near = [d for d in cores if d != core and topo.may_write(core, d)]
+    mine = [st for st in streams if st[0] == rank]
+
+    def bank(b):
+        return T.ps[:, 512 * b:512 * b + NC]
+
+    def blk(j):
+        return slice(NC * j, NC * j + NC)
+
+    a.dma_start(T.xk_t[:], T.xk[:]).then_inc(S.ld_xk, 16)
+    sy.dma_start(T.wk_t[:], T.wk[:]).then_inc(S.ld_wk, 16)
+    a.dma_start(T.xq_t[:], T.xq[:]).then_inc(S.ld_xq, 16)
+    sy.dma_start(T.wq_t[:], T.wq[:]).then_inc(S.ld_wq, 16)
+
+    def project(n, b0, out_c, out_s):
+        x_t, w_t, x_c, x_s, w_c, w_s = (T[s % n] for s in ("x%s_t", "w%s_t", "x%s_c", "x%s_s", "w%s_c", "w%s_s"))
+        tile = T["%s_t" % n]
+        v.wait_ge(S["ld_x" + n], 16)
+        v.quantize_mx(x_c[:], x_s[:], x_t[:]).then_inc(S["qx" + n], 1)
+        v.wait_ge(S["ld_w" + n], 16)
+        t.wait_ge(S["qx" + n], 1)
+        for i in range(2):
+            v.quantize_mx(w_c[:, blk(i)], w_s[:, blk(i)], w_t[:, 512 * i:512 * i + 512]).then_inc(S["qw%d%s" % (i, n)], 1)
+            t.wait_ge(S["qw%d%s" % (i, n)], 1)
+            t.matmul_mx(bank(b0 + i), w_c[:, blk(i)], w_s[:, blk(i)], x_c[:], x_s[:], True, True).then_inc(S["z%d%s" % (i, n)], 1)
+        v.wait_ge(S["z0" + n], 1)
+        v.tensor_scalar(tile[:, 0:512:4], bank(b0), C, 0.0, AluOpType.mult, AluOpType.max).then_inc(S["av" + n], 1)
+        v.tensor_scalar(tile[:, 1:512:4], bank(b0), -C, 0.0, AluOpType.mult, AluOpType.max).then_inc(S["av" + n], 1)
+        a.wait_ge(S["z1" + n], 1)
+        a.activation(tile[:, 2:512:4], bank(b0 + 1), ActivationFunctionType.Relu, scale=C).then_inc(S["as" + n], 1)
+        a.activation(tile[:, 3:512:4], bank(b0 + 1), ActivationFunctionType.Relu, scale=-C).then_inc(S["as" + n], 1)
+        v.wait_ge(S["av" + n], 2)
+        v.wait_ge(S["as" + n], 2)
+        v.quantize_mx(out_c, out_s, tile[:]).then_inc(S["done" + n], 1)
+
+    project("k", 0, T.kc[:, blk(rank)], T.ks[:, blk(rank)])
+
+    g.wait_ge(S.donek, 1)
+    left = 0
+    busy = 0
+    for j, p, relay, far in mine:
+        m = off_mask(core, [relay])
+        rid, pid = topo.addr(relay, core)
+        g.remote_dma(piece(p, rank), piece(p, rank), S["arr%d" % rank], S.left, pid, rid, m)
+        left += count(m)
+        busy |= m
+    for d in near:
+        m = engines(topo.mask(core, d), ENG_ON, busy)
+        rid, pid = topo.addr(d, core)
+        for codes in (True, False):
+            g.remote_dma(view(codes, rank, 0, NC), view(codes, rank, 0, NC), S["arr%d" % rank], S.left, pid, rid, m)
+            left += count(m)
+
+    project("q", 2, T.qc[:], T.qs[:])
+
+    def expected(j):
+        if cores[j] in near:
+            return 2 * count(engines(topo.mask(cores[j], core), ENG_ON))
+        return sum(count(off_mask(relay, far)) for jj, p, relay, far in streams if jj == j)
+
+    home = sorted([rank] + [cores.index(d) for d in near])
+    away = [j for j in range(len(cores)) if j not in home]
+    t.wait_ge(S.doneq, 1)
+    t.wait_ge(S.donek, 1)
+    for n, j in enumerate([rank] + [j for j in home if j != rank] + away):
+        if j != rank:
+            t.wait_ge(S["arr%d" % j], expected(j))
+        t.matmul_mx(bank(4 + j), T.kc[:, blk(j)], T.ks[:, blk(j)], T.qc[:], T.qs[:], True, True).then_inc(S["y%d" % j], 1)
+        if n % 2 == 0:
+            v.wait_ge(S["y%d" % j], 1)
+            v.tensor_copy(T.y_t[:, blk(j)], bank(4 + j)).then_inc(S["c%d" % j], 1)
+        else:
+            a.wait_ge(S["y%d" % j], 1)
+            a.activation(T.y_t[:, blk(j)], bank(4 + j), ActivationFunctionType.Copy).then_inc(S["c%d" % j], 1)
+
+    stores = []
+    for j in home:
+        sy.wait_ge(S["c%d" % j], 1)
+    lo, hi = NC * home[0], NC * home[-1] + NC
+    sy.dma_start(T.y[:, lo:hi], T.y_t[:, lo:hi]).then_inc(S["st%d" % home[0]], 16)
+    stores.append(home[0])
+    for n, j in enumerate(away):
+        q = sy if n % 2 == 0 else a
+        q.wait_ge(S["c%d" % j], 1)
+        q.dma_start(T.y[:, blk(j)], T.y_t[:, blk(j)]).then_inc(S["st%d" % j], 16)
+        stores.append(j)
+
+    g.wait_ge(S.left, left)
+    for j in stores:
+        g.wait_ge(S["st%d" % j], 16)

@@ -5,8 +5,13 @@ from concourse.mybir import dt, AluOpType, ActivationFunctionType
 NC = 128
 HOSTS = 4
 C = float(np.float32(0.031))
+Q4 = NC // 4
 
-PIECES = [(True, 0, NC, False), (False, 0, NC, True)]
+PIECES = [(True, 0, Q4, False, None, 0, 4),
+          (True, Q4, 3 * Q4, False, 0, 0, 4),
+          (True, 3 * Q4, NC, True, None, 4, 2),
+          (False, 0, NC, True, None, 6, 2)]
+CALLS = [[0, 2, 3], [1]]
 ENG_OFF = 8
 ENG_ON = 8
 
@@ -24,14 +29,14 @@ SCRATCH = {
     "ps": ("psum", [128, 8 * 512], "float32"),
 }
 SEMAPHORES = ([s + n for n in "kq" for s in ("ld_x", "ld_w", "qx", "qw0", "qw1", "z0", "z1", "av", "as", "done")]
-              + [s + str(j) for s in ("arr", "y", "c", "st") for j in range(4)] + ["left"])
+              + [s + str(j) for s in ("arr", "y", "c", "st", "in") for j in range(4)] + ["left"])
 
 
-def engines(mask, n, avoid=0):
+def engines(mask, n, avoid=0, first=0):
     free = [i for i in range(mask.bit_length()) if (mask >> i) & 1]
     order = [i for i in free if not (avoid >> i) & 1] + [i for i in free if (avoid >> i) & 1]
     m = 0
-    for i in order[:n]:
+    for i in order[first:first + n]:
         m |= 1 << i
     return m
 
@@ -41,19 +46,34 @@ def count(mask):
 
 
 def plan(cores, topo):
+    world = range(HOSTS * topo.CORES_PER_HOST)
+
+    def way_out(c, cable):
+        if not cable:
+            return (topo.host(c), topo.die(c))
+        return (topo.host(c), topo.die(c), any(topo.may_write(c, m) for m in world if topo.mates(c, m)))
+
     used = set(cores)
+    load = {}
     streams = []
     for j, s in enumerate(cores):
         far = [d for d in cores if d != s and not topo.may_write(s, d)]
         if not far:
             continue
-        for p, (_, _, _, own_rack) in enumerate(PIECES):
-            ok = [c for c in range(HOSTS * topo.CORES_PER_HOST)
-                  if c not in used and topo.chip(c) == topo.chip(s) and topo.die(c) == topo.die(s)
-                  and topo.may_write(s, c) and all(topo.may_write(c, d) for d in far)
-                  and (topo.same_plane(s, c) if own_rack else all(topo.same_plane(c, d) for d in far))]
-            used.add(ok[0])
-            streams.append((j, p, ok[0], far))
+        chosen = {}
+        for p, (codes, lo, hi, own_rack, shares, _, _) in enumerate(PIECES):
+            if shares is None:
+                ok = [c for c in world
+                      if c not in used and topo.chip(c) == topo.chip(s)
+                      and topo.may_write(s, c) and all(topo.may_write(c, d) for d in far)
+                      and (topo.same_plane(s, c) if own_rack else all(topo.same_plane(c, d) for d in far))]
+                relay = min(ok, key=lambda c: (load.get(way_out(c, own_rack), 0), topo.die(c) != topo.die(s), c))
+            else:
+                relay = chosen[shares]
+            chosen[p] = relay
+            used.add(relay)
+            load[way_out(relay, own_rack)] = load.get(way_out(relay, own_rack), 0) + (hi - lo) * (4 if codes else 1)
+            streams.append((j, p, relay, far))
     return streams
 
 
@@ -77,22 +97,28 @@ def rank_program(g, core, T, topo):
             m &= topo.mask(src, d)
         return engines(m, ENG_OFF)
 
+    def first_hop(src, p, relay):
+        return engines(topo.mask(src, relay), PIECES[p][6], 0, PIECES[p][5])
+
     if rank is None:
+        left = 0
         for j, p, relay, far in streams:
             if relay != core:
                 continue
             m = off_mask(core, far)
             ids = [DstId(rid=topo.addr(d, core)[0], pnc=topo.addr(d, core)[1]) for d in far]
-            g.wait_ge(S["arr%d" % j], count(off_mask(cores[j], [relay])))
+            g.wait_ge(S["in%d" % p], count(first_hop(cores[j], p, relay)))
             g.remote_dma_fused([RemoteDMATransfer(dst_ids=ids, dma_engine_mask=m, remote_sem=S["arr%d" % j],
                                                   srcs=[piece(p, j)], dsts=[piece(p, j) for _ in far])],
                                local_sem=S.left)
-            g.wait_ge(S.left, count(m))
+            left += count(m)
+        if left:
+            g.wait_ge(S.left, left)
         return
 
     v, a, t, sy = g.vector, g.scalar, g.tensor, g.sync
     near = [d for d in cores if d != core and topo.may_write(core, d)]
-    mine = [st for st in streams if st[0] == rank]
+    mine = dict((p, relay) for j, p, relay, far in streams if j == rank)
 
     def bank(b):
         return T.ps[:, 512 * b:512 * b + NC]
@@ -116,14 +142,14 @@ def rank_program(g, core, T, topo):
             v.quantize_mx(w_c[:, blk(i)], w_s[:, blk(i)], w_t[:, 512 * i:512 * i + 512]).then_inc(S["qw%d%s" % (i, n)], 1)
             t.wait_ge(S["qw%d%s" % (i, n)], 1)
             t.matmul_mx(bank(b0 + i), w_c[:, blk(i)], w_s[:, blk(i)], x_c[:], x_s[:], True, True).then_inc(S["z%d%s" % (i, n)], 1)
-        v.wait_ge(S["z0" + n], 1)
-        v.tensor_scalar(tile[:, 0:512:4], bank(b0), C, 0.0, AluOpType.mult, AluOpType.max).then_inc(S["av" + n], 1)
-        v.tensor_scalar(tile[:, 1:512:4], bank(b0), -C, 0.0, AluOpType.mult, AluOpType.max).then_inc(S["av" + n], 1)
-        a.wait_ge(S["z1" + n], 1)
-        a.activation(tile[:, 2:512:4], bank(b0 + 1), ActivationFunctionType.Relu, scale=C).then_inc(S["as" + n], 1)
-        a.activation(tile[:, 3:512:4], bank(b0 + 1), ActivationFunctionType.Relu, scale=-C).then_inc(S["as" + n], 1)
-        v.wait_ge(S["av" + n], 2)
+        a.wait_ge(S["z0" + n], 1)
+        a.activation(tile[:, 0:512:4], bank(b0), ActivationFunctionType.Relu, scale=C).then_inc(S["as" + n], 1)
+        a.activation(tile[:, 1:512:4], bank(b0), ActivationFunctionType.Relu, scale=-C).then_inc(S["as" + n], 1)
+        v.wait_ge(S["z1" + n], 1)
+        v.tensor_scalar(tile[:, 2:512:4], bank(b0 + 1), C, 0.0, AluOpType.mult, AluOpType.max).then_inc(S["av" + n], 1)
+        v.tensor_scalar(tile[:, 3:512:4], bank(b0 + 1), -C, 0.0, AluOpType.mult, AluOpType.max).then_inc(S["av" + n], 1)
         v.wait_ge(S["as" + n], 2)
+        v.wait_ge(S["av" + n], 2)
         v.quantize_mx(out_c, out_s, tile[:]).then_inc(S["done" + n], 1)
 
     project("k", 0, T.kc[:, blk(rank)], T.ks[:, blk(rank)])
@@ -131,12 +157,16 @@ def rank_program(g, core, T, topo):
     g.wait_ge(S.donek, 1)
     left = 0
     busy = 0
-    for j, p, relay, far in mine:
-        m = off_mask(core, [relay])
-        rid, pid = topo.addr(relay, core)
-        g.remote_dma(piece(p, rank), piece(p, rank), S["arr%d" % rank], S.left, pid, rid, m)
-        left += count(m)
-        busy |= m
+    for call in CALLS:
+        transfers = []
+        for p in call:
+            m = first_hop(core, p, mine[p])
+            rid, pid = topo.addr(mine[p], core)
+            transfers.append(RemoteDMATransfer(dst_ids=[DstId(rid=rid, pnc=pid)], dma_engine_mask=m,
+                                               remote_sem=S["in%d" % p], srcs=[piece(p, rank)], dsts=[piece(p, rank)]))
+            left += count(m)
+            busy |= m
+        g.remote_dma_fused(transfers, local_sem=S.left)
     for d in near:
         m = engines(topo.mask(core, d), ENG_ON, busy)
         rid, pid = topo.addr(d, core)

import numpy as np
from concourse.bass import DstId, RemoteDMATransfer
from concourse.mybir import dt, AluOpType, ActivationFunctionType

NC = 128
HOSTS = 4
C = float(np.float32(0.031))
Q4 = NC // 4

PIECES = [(True, 0, Q4, False, None, 0, 4),
          (True, Q4, 3 * Q4, False, 0, 0, 4),
          (True, 3 * Q4, NC, True, None, 4, 2),
          (False, 0, NC, True, None, 6, 2)]
CALLS = [[0, 2, 3], [1]]
ENG_OFF = 8
ENG_ON = 8

SCRATCH = {
    "xk_t": ("sbuf", [128, 512], "bfloat16"), "wk_t": ("sbuf", [128, 1024], "bfloat16"),
    "xq_t": ("sbuf", [128, 512], "bfloat16"), "wq_t": ("sbuf", [128, 1024], "bfloat16"),
    "xk_c": ("sbuf", [128, NC], "float8_e4m3fn_x4"), "xk_s": ("sbuf", [128, NC], "uint8"),
    "xq_c": ("sbuf", [128, NC], "float8_e4m3fn_x4"), "xq_s": ("sbuf", [128, NC], "uint8"),
    "wk_c": ("sbuf", [128, 2 * NC], "float8_e4m3fn_x4"), "wk_s": ("sbuf", [128, 2 * NC], "uint8"),
    "wq_c": ("sbuf", [128, 2 * NC], "float8_e4m3fn_x4"), "wq_s": ("sbuf", [128, 2 * NC], "uint8"),
    "k_t": ("sbuf", [128, 512], "bfloat16"), "q_t": ("sbuf", [128, 512], "bfloat16"),
    "kc": ("sbuf", [128, 4 * NC], "float8_e4m3fn_x4"), "ks": ("sbuf", [128, 4 * NC], "uint8"),
    "qc": ("sbuf", [128, NC], "float8_e4m3fn_x4"), "qs": ("sbuf", [128, NC], "uint8"),
    "y_t": ("sbuf", [128, 4 * NC], "float32"),
    "ps": ("psum", [128, 8 * 512], "float32"),
}
SEMAPHORES = ([s + n for n in "kq" for s in ("ld_x", "ld_w", "qx", "qw0", "qw1", "z0", "z1", "av", "as", "done")]
              + [s + str(j) for s in ("arr", "y", "c", "st", "in") for j in range(4)] + ["left"])


def engines(mask, n, avoid=0, first=0):
    free = [i for i in range(mask.bit_length()) if (mask >> i) & 1]
    order = [i for i in free if not (avoid >> i) & 1] + [i for i in free if (avoid >> i) & 1]
    m = 0
    for i in order[first:first + n]:
        m |= 1 << i
    return m


def count(mask):
    return bin(mask).count("1")


def plan(cores, topo):
    world = range(HOSTS * topo.CORES_PER_HOST)

    def way_out(c, cable):
        if not cable:
            return (topo.host(c), topo.die(c))
        return (topo.host(c), topo.die(c), any(topo.may_write(c, m) for m in world if topo.mates(c, m)))

    used = set(cores)
    load = {}
    streams = []
    for j, s in enumerate(cores):
        far = [d for d in cores if d != s and not topo.may_write(s, d)]
        if not far:
            continue
        chosen = {}
        for p, (codes, lo, hi, own_rack, shares, _, _) in enumerate(PIECES):
            if shares is None:
                ok = [c for c in world
                      if c not in used and topo.chip(c) == topo.chip(s)
                      and topo.may_write(s, c) and all(topo.may_write(c, d) for d in far)
                      and (topo.same_plane(s, c) if own_rack else all(topo.same_plane(c, d) for d in far))]
                relay = min(ok, key=lambda c: (load.get(way_out(c, own_rack), 0), topo.die(c) != topo.die(s), c))
            else:
                relay = chosen[shares]
            chosen[p] = relay
            used.add(relay)
            load[way_out(relay, own_rack)] = load.get(way_out(relay, own_rack), 0) + (hi - lo) * (4 if codes else 1)
            streams.append((j, p, relay, far))
    return streams


def rank_program(g, core, T, topo):
    cores = [int(c) for c in T.cores]
    streams = plan(cores, topo)
    S = T.sem
    rank = T.rank_of(core)

    def view(codes, j, lo, hi):
        if codes:
            return T.kc[:, NC * j + lo:NC * j + hi].bitcast(dt.uint8)
        return T.ks[:, NC * j + lo:NC * j + hi]

    def piece(p, j):
        return view(PIECES[p][0], j, PIECES[p][1], PIECES[p][2])

    def off_mask(src, dsts):
        m = topo.mask(src, dsts[0])
        for d in dsts[1:]:
            m &= topo.mask(src, d)
        return engines(m, ENG_OFF)

    def first_hop(src, p, relay):
        return engines(topo.mask(src, relay), PIECES[p][6], 0, PIECES[p][5])

    if rank is None:
        left = 0
        for j, p, relay, far in streams:
            if relay != core:
                continue
            m = off_mask(core, far)
            ids = [DstId(rid=topo.addr(d, core)[0], pnc=topo.addr(d, core)[1]) for d in far]
            g.wait_ge(S["in%d" % p], count(first_hop(cores[j], p, relay)))
            g.remote_dma_fused([RemoteDMATransfer(dst_ids=ids, dma_engine_mask=m, remote_sem=S["arr%d" % j],
                                                  srcs=[piece(p, j)], dsts=[piece(p, j) for _ in far])],
                               local_sem=S.left)
            left += count(m)
        if left:
            g.wait_ge(S.left, left)
        return

    v, a, t, sy = g.vector, g.scalar, g.tensor, g.sync
    near = [d for d in cores if d != core and topo.may_write(core, d)]
    mine = dict((p, relay) for j, p, relay, far in streams if j == rank)

    def bank(b):
        return T.ps[:, 512 * b:512 * b + NC]

    def blk(j):
        return slice(NC * j, NC * j + NC)

    a.dma_start(T.xk_t[:], T.xk[:]).then_inc(S.ld_xk, 16)
    sy.dma_start(T.wk_t[:], T.wk[:]).then_inc(S.ld_wk, 16)
    a.dma_start(T.xq_t[:], T.xq[:]).then_inc(S.ld_xq, 16)
    sy.dma_start(T.wq_t[:], T.wq[:]).then_inc(S.ld_wq, 16)

    def project(n, b0, out_c, out_s):
        x_t, w_t, x_c, x_s, w_c, w_s = (T[s % n] for s in ("x%s_t", "w%s_t", "x%s_c", "x%s_s", "w%s_c", "w%s_s"))
        tile = T["%s_t" % n]
        v.wait_ge(S["ld_x" + n], 16)
        v.quantize_mx(x_c[:], x_s[:], x_t[:]).then_inc(S["qx" + n], 1)
        v.wait_ge(S["ld_w" + n], 16)
        t.wait_ge(S["qx" + n], 1)
        for i in range(2):
            v.quantize_mx(w_c[:, blk(i)], w_s[:, blk(i)], w_t[:, 512 * i:512 * i + 512]).then_inc(S["qw%d%s" % (i, n)], 1)
            t.wait_ge(S["qw%d%s" % (i, n)], 1)
            t.matmul_mx(bank(b0 + i), w_c[:, blk(i)], w_s[:, blk(i)], x_c[:], x_s[:], True, True).then_inc(S["z%d%s" % (i, n)], 1)
        a.wait_ge(S["z0" + n], 1)
        a.activation(tile[:, 0:512:4], bank(b0), ActivationFunctionType.Relu, scale=C).then_inc(S["as" + n], 1)
        a.activation(tile[:, 1:512:4], bank(b0), ActivationFunctionType.Relu, scale=-C).then_inc(S["as" + n], 1)
        v.wait_ge(S["z1" + n], 1)
        v.tensor_scalar(tile[:, 2:512:4], bank(b0 + 1), C, 0.0, AluOpType.mult, AluOpType.max).then_inc(S["av" + n], 1)
        v.tensor_scalar(tile[:, 3:512:4], bank(b0 + 1), -C, 0.0, AluOpType.mult, AluOpType.max).then_inc(S["av" + n], 1)
        v.wait_ge(S["as" + n], 2)
        v.wait_ge(S["av" + n], 2)
        v.quantize_mx(out_c, out_s, tile[:]).then_inc(S["done" + n], 1)

    project("k", 0, T.kc[:, blk(rank)], T.ks[:, blk(rank)])

    g.wait_ge(S.donek, 1)
    left = 0
    busy = 0
    for call in CALLS:
        transfers = []
        for p in call:
            m = first_hop(core, p, mine[p])
            rid, pid = topo.addr(mine[p], core)
            transfers.append(RemoteDMATransfer(dst_ids=[DstId(rid=rid, pnc=pid)], dma_engine_mask=m,
                                               remote_sem=S["in%d" % p], srcs=[piece(p, rank)], dsts=[piece(p, rank)]))
            left += count(m)
            busy |= m
        g.remote_dma_fused(transfers, local_sem=S.left)
    for d in near:
        m = engines(topo.mask(core, d), ENG_ON, busy)
        rid, pid = topo.addr(d, core)
        for codes in (True, False):
            g.remote_dma(view(codes, rank, 0, NC), view(codes, rank, 0, NC), S["arr%d" % rank], S.left, pid, rid, m)
            left += count(m)

    project("q", 2, T.qc[:], T.qs[:])

    def expected(j):
        if cores[j] in near:
            return 2 * count(engines(topo.mask(cores[j], core), ENG_ON))
        return sum(count(off_mask(relay, far)) for jj, p, relay, far in streams if jj == j)

    home = sorted([rank] + [cores.index(d) for d in near])
    away = [j for j in range(len(cores)) if j not in home]
    t.wait_ge(S.doneq, 1)
    t.wait_ge(S.donek, 1)
    for n, j in enumerate([rank] + [j for j in home if j != rank] + away):
        if j != rank:
            t.wait_ge(S["arr%d" % j], expected(j))
        t.matmul_mx(bank(4 + j), T.kc[:, blk(j)], T.ks[:, blk(j)], T.qc[:], T.qs[:], True, True).then_inc(S["y%d" % j], 1)
        if n % 2 == 0:
            v.wait_ge(S["y%d" % j], 1)
            v.tensor_copy(T.y_t[:, blk(j)], bank(4 + j)).then_inc(S["c%d" % j], 1)
        else:
            a.wait_ge(S["y%d" % j], 1)
            a.activation(T.y_t[:, blk(j)], bank(4 + j), ActivationFunctionType.Copy).then_inc(S["c%d" % j], 1)

    stores = []
    for j in home:
        sy.wait_ge(S["c%d" % j], 1)
    lo, hi = NC * home[0], NC * home[-1] + NC
    sy.dma_start(T.y[:, lo:hi], T.y_t[:, lo:hi]).then_inc(S["st%d" % home[0]], 16)
    stores.append(home[0])
    for n, j in enumerate(away):
        q = sy if n % 2 == 0 else a
        q.wait_ge(S["c%d" % j], 1)
        q.dma_start(T.y[:, blk(j)], T.y_t[:, blk(j)]).then_inc(S["st%d" % j], 16)
        stores.append(j)

    g.wait_ge(S.left, left)
    for j in stores:
        g.wait_ge(S["st%d" % j], 16)
